import numpy as np
import ml_dtypes


def mxq(x, axis, fmt="e4m3"):
    dtype, down = {"e4m3": (ml_dtypes.float8_e4m3fn, 7), "e5m2": (ml_dtypes.float8_e5m2, 14)}[fmt]
    v = np.moveaxis(np.asarray(x, np.float32).astype(ml_dtypes.bfloat16).astype(np.float64), axis, -1)
    blocks = v.reshape(v.shape[:-1] + (-1, 32))
    amax = np.abs(blocks).max(-1, keepdims=True)
    byte = np.maximum(np.where(amax > 0, np.frexp(amax)[1] - 1 + 127, 0) - down, 1)
    scale = np.exp2(byte - 127.0)
    codes = (blocks / scale).astype(np.float32).astype(dtype).astype(np.float64)
    return np.moveaxis((codes * scale).reshape(v.shape), -1, axis)


WIDE = False


def mx_kscale(k):
    if not WIDE:
        return np.ones(k)
    levels = np.array([10, -10, 5, -5, 0])
    if k % 512:
        return np.exp2(np.random.permutation(np.resize(levels, k // 32))).repeat(32)
    a = np.empty((k // 512, 16))
    for p in range(k // 512):
        a[p, :8] = np.random.permutation(np.resize(levels, 8))
        for g in range(8):
            far = levels[np.abs(levels - a[p, g]) >= 10]
            a[p, g + 8] = far[np.random.randint(len(far))]
    return np.exp2(a.ravel()).repeat(32)


def f64(x):
    return np.asarray(x).astype(np.float64)


def striped(idx):
    return np.tile(idx.reshape(-1, 16).T, (8, 1)).astype(np.uint16)


def unstriped(offs):
    return offs[:16].T.reshape(-1).astype(np.int64)


def striped8(idx):
    return np.concatenate([x.reshape(-1, 16).T for x in idx]).astype(np.uint16)


def runs(offs, k):
    lists = np.stack([offs[16 * r : 16 * r + 16].T.reshape(-1) for r in range(8)]).astype(np.int64)
    return lists[np.arange(k) % 512 // 64]


def pack_weight(w):
    k, n = w.shape
    w = f64(np.asarray(w, np.float32).astype(ml_dtypes.bfloat16)).reshape(k // 32, 32, n)
    amax = np.abs(w).max(1)
    byte = np.clip(np.where(amax > 0, np.frexp(amax)[1] - 1 + 127 - 7, 1), 1, 254)
    scaled = (w * np.exp2(127.0 - byte)[:, None, :]).reshape(k, n).astype(np.float32)
    words = np.ascontiguousarray(scaled.reshape(k // 512, 128, 4, n).transpose(0, 1, 3, 2)).astype(ml_dtypes.float8_e4m3fn).view(np.uint8)
    return words, np.ascontiguousarray(byte.astype(np.uint8).reshape(k // 512, 16, n))


def unpack_weight(words, scales):
    g, p, n, _ = words.shape
    vals = np.ascontiguousarray(words).view(ml_dtypes.float8_e4m3fn).astype(np.float64) * np.repeat(np.exp2(scales.astype(np.float64) - 127.0), 8, axis=1)[..., None]
    return vals.transpose(0, 1, 3, 2).reshape(g * 512, n)


def sigmoid(v):
    return 1.0 / (1.0 + np.exp(-np.maximum(v, -700.0)))


K, T, S, N, H, U = 512, 2048, 512, 512, 512, 1024


def setup_inputs():
    n = np.random.standard_normal
    s = mx_kscale(K)[:, None]
    u = mx_kscale(H)
    packed_xT = pack_weight(n((K, T)) * s)
    return {
        "x_words": packed_xT[0],
        "x_scales": packed_xT[1],
        "w1": (n((K, H)) / np.sqrt(K) / s).astype(np.float32),
        "w2": (n((K, H)) / np.sqrt(K) / s).astype(np.float32),
        "sl": np.random.uniform(1.0, 2.0, (H, 1)).astype(np.float32),
        "th": (0.5 * n((H, 1))).astype(np.float32),
        "sl2": np.random.uniform(1.0, 2.0, (H, 1)).astype(np.float32),
        "th2": (0.5 * n((H, 1))).astype(np.float32),
        "gn": (np.random.uniform(0.5, 1.5, (H, 1)) * u[:, None]).astype(np.float32),
        "w3": (n((H, N)) / np.sqrt(H) / u[:, None]).astype(np.float32),
        "mem": n((N, U)).astype(np.float32),
        "offs": striped(np.random.permutation(T)[:S]),
        "hz": striped8(np.random.randint(0, T, (8, S))),
        "n1": striped(np.random.permutation(S)),
        "n2": striped(np.random.permutation(S)),
        "n3": striped(np.random.permutation(U)[:S]),
    }


def reference(x_words, x_scales, w1, w2, sl, th, sl2, th2, gn, w3, mem, offs, hz, n1, n2, n3):
    old = f64(mem)[:, unstriped(n3)]
    xq = unpack_weight(x_words, x_scales)[:, unstriped(offs)]
    y = mxq(f64(w1), 0, "e4m3").T @ xq
    sg = sigmoid(f64(sl) * (y[:, unstriped(n1)] - f64(th)))
    x_hz = unpack_weight(x_words, x_scales)[np.arange(K)[:, None], runs(hz, K)]
    d = mxq(f64(w2), 0, "e4m3").T @ x_hz
    sg2 = sigmoid(f64(sl2) * (d[:, unstriped(n2)] - f64(th2)))
    z = f64(gn) * (sg * d + sg2 * y)
    h = mxq(f64(w3), 0, "e4m3").T @ mxq(z, 0, "e4m3")
    nw = old + sigmoid(h) * (h - old)
    out = f64(mem).copy()
    out[:, unstriped(n3)] = nw
    return out

@@ -1,0 +1,227 @@
+from contextlib import ExitStack
+
+import concourse.mybir as mybir
+
+K, T, S, N, H, U = 512, 2048, 512, 512, 512, 1024
+FLOPS = 2 * S * (2 * K * H + H * N)
+
+F32 = mybir.dt.float32
+BF16 = mybir.dt.bfloat16
+I32 = mybir.dt.int32
+U32 = mybir.dt.uint32
+U16 = mybir.dt.uint16
+U8 = mybir.dt.uint8
+FP8X4 = mybir.dt.float8_e4m3fn_x4
+ALU = mybir.AluOpType
+ACT = mybir.ActivationFunctionType
+
+P = 128
+PACK = 4
+HALF = 256
+LIST_COLS = S // 16
+
+
+def tile_picked_twhcxbpaget_none_p_kernel(tc, x_words, x_scales, w1, w2, sl, th, sl2, th2, gn, w3, mem, offs, hz, n1, n2, n3, out):
+    nc = tc.nc
+    with ExitStack() as ctx:
+        lists = ctx.enter_context(tc.tile_pool(name="lists", bufs=1))
+        sb = ctx.enter_context(tc.tile_pool(name="sb", bufs=1))
+        psum = ctx.enter_context(tc.psum_pool(name="psum", bufs=1))
+
+        def tile(shape, dtype, name, tag=None):
+            return sb.tile(shape, dtype, name=name, tag=tag or name, align_bytes=64)
+
+        def load_list(src, name):
+            t = lists.tile([P, LIST_COLS], U16, name=name)
+            nc.sync.dma_start(t[:], src)
+            return t
+
+        def half_of(lst, c):
+            return lst[:, c * LIST_COLS // 2 : (c + 1) * LIST_COLS // 2]
+
+        def cols(c):
+            return slice(c * HALF, (c + 1) * HALF)
+
+        scale_win = tile([P, T], U8, "scale_win", tag="stage_a")
+        nc.gpsimd.memset(scale_win[:].bitcast(I32), 0)
+        for e in range(2):
+            nc.scalar.dma_start(scale_win[:].bitcast(I32)[e:P:16, :], x_scales[0].bitcast(I32)[e:16:2, :])
+        for e in range(2, 4):
+            nc.scalar.dma_start(scale_win[:].bitcast(I32)[e:P:32, :], x_scales[0].bitcast(I32)[e:16:4, :])
+
+        offs_l = load_list(offs, "offs_l")
+        hz_l = load_list(hz, "hz_l")
+
+        word_win = tile([P, T], I32, "word_win", tag="stage_b")
+        nc.sync.dma_start(word_win[:], x_words[0].rearrange("p n t -> p (n t)").bitcast(I32))
+
+        def load_w_half(w, c, name, tag):
+            raw = tile([P, PACK, HALF], F32, name, tag=tag)
+            nc.sync.dma_start(raw[:], w.rearrange("(p j) c -> p j c", j=PACK)[:, :, cols(c)])
+            return raw
+
+        w1_raw = [load_w_half(w1, c, f"w1_raw{c}", f"stage_c{c}") for c in range(2)]
+        w2_raw = [load_w_half(w2, c, f"w2_raw{c}", f"stage_d{c}") for c in range(2)]
+
+        n1_l = load_list(n1, "n1_l")
+        n2_l = load_list(n2, "n2_l")
+        n3_l = load_list(n3, "n3_l")
+
+        def load_rows(v, name):
+            t = tile([P, PACK], F32, name)
+            nc.gpsimd.dma_start(t[:], v.rearrange("(p t) o -> p (t o)", t=PACK))
+            return t
+
+        sl_t = load_rows(sl, "sl_t")
+        th_t = load_rows(th, "th_t")
+        sl2_t = load_rows(sl2, "sl2_t")
+        th2_t = load_rows(th2, "th2_t")
+        gn_t = load_rows(gn, "gn_t")
+
+        tok_plane = tile([P, S], U8, "tok_plane")
+        hash_bytes = tile([P, S], U8, "hash_bytes")
+        hash_plane = tile([P, S], U8, "hash_plane")
+        nc.vector.tensor_copy(tok_plane[:], scale_win[:].indirect(offs_l[:]))
+        nc.vector.tensor_copy(hash_bytes[:], scale_win[:].indirect(hz_l[:]))
+        nc.vector.tensor_copy(hash_plane[:].bitcast(I32), hash_bytes[:].bitcast(I32))
+        for e in range(2):
+            nc.gpsimd.dma_start(hash_plane[:].bitcast(I32)[2 + e : P : 32, :], hash_bytes[:].bitcast(I32)[16 + e : P : 32, :])
+        x_tok = tile([P, S], U32, "x_tok")
+        x_hash = tile([P, S], U32, "x_hash")
+        nc.vector.tensor_copy(x_tok[:], word_win[:].bitcast(U32).indirect(offs_l[:]))
+        nc.vector.tensor_copy(x_hash[:], word_win[:].bitcast(U32).indirect(hz_l[:]))
+
+        bias1 = tile([P, PACK], F32, "bias1")
+        bias2 = tile([P, PACK], F32, "bias2")
+        nc.vector.scalar_tensor_tensor(bias1[:], sl_t[:], -1.0, th_t[:], ALU.mult, ALU.mult)
+        nc.vector.scalar_tensor_tensor(bias2[:], sl2_t[:], -1.0, th2_t[:], ALU.mult, ALU.mult)
+
+        def round_dealt(copy, grouped, raw, c):
+            m = slice(c * HALF // PACK, (c + 1) * HALF // PACK)
+            copy(grouped[:, :, m, :].rearrange("p t m j -> p m j t"), raw[:].rearrange("p j (m t) -> p m j t", t=PACK))
+
+        def gpsimd_round(dst, src):
+            nc.gpsimd.tensor_scalar(dst, src, 1.0, 0.0, ALU.mult, ALU.add)
+
+        def quantise(grouped_flat, width, name, pieces):
+            codes = tile([P, width], U32, name + "_codes")
+            plane = tile([P, width], U8, name + "_plane")
+            step = width // pieces
+            for i in range(pieces):
+                s = slice(i * step, (i + 1) * step)
+                nc.vector.quantize_mx(codes[:, s].bitcast(FP8X4), plane[:, s], grouped_flat[:, PACK * i * step : PACK * (i + 1) * step])
+            return codes, plane
+
+        def project(codes, plane, t, x, x_scale, bank):
+            m = slice(t * P, (t + 1) * P)
+            nc.tensor.matmul_mx(bank, lhsT=codes[:, m].bitcast(FP8X4), lhsT_scale=plane[:, m], rhs=x.bitcast(FP8X4), rhs_scale=x_scale, start=True, stop=True)
+
+        w1_bf = tile([P, PACK, P, PACK], BF16, "w1_bf")
+        round_dealt(nc.scalar.copy, w1_bf, w1_raw[0], 0)
+        round_dealt(nc.scalar.copy, w1_bf, w1_raw[1], 1)
+        w1_codes, w1_plane = quantise(w1_bf[:].rearrange("p t m j -> p (t m j)"), H, "w1", 2)
+
+        y = [tile([P, S], F32, f"y{t}") for t in range(PACK)]
+        d = [tile([P, S], F32, f"d{t}") for t in range(PACK)]
+        y_bank = [psum.tile([P, S], F32, name=f"y_bank{t}", tag=f"bank{t}") for t in range(PACK)]
+        d_bank = [psum.tile([P, S], F32, name=f"d_bank{t}", tag=f"bank{PACK + t}") for t in range(PACK)]
+        for t in range(PACK):
+            project(w1_codes, w1_plane, t, x_tok[:], tok_plane[:], y_bank[t][:])
+
+        w2_bf = tile([P, PACK, P, PACK], BF16, "w2_bf", tag="w_bf")
+        round_dealt(nc.scalar.copy, w2_bf, w2_raw[0], 0)
+        round_dealt(nc.vector.tensor_copy, w2_bf, w2_raw[1], 1)
+        w2_codes, w2_plane = quantise(w2_bf[:].rearrange("p t m j -> p (t m j)"), H, "w2", 2)
+        for t in range(PACK):
+            project(w2_codes, w2_plane, t, x_hash[:], hash_plane[:], d_bank[t][:])
+
+        w3_raw = [load_w_half(w3, 0, "w3_raw0", "stage_c0"), load_w_half(w3, 1, "w3_raw1", "stage_b")]
+        page = []
+        for m, tag in enumerate(("stage_c1", "stage_a", "stage_d0", "stage_d1")):
+            pg = tile([P, U], F32, f"page{m}", tag=tag)
+            nc.sync.dma_start(pg[:], mem[m * P : (m + 1) * P, :])
+            page.append(pg)
+
+        def gate(name, src, lst, slope, bias, t, c):
+            dst = tile([P, HALF], F32, f"{name}{c}{t}", tag=f"{name}{t}")
+            nc.scalar.activation(dst[:], src[t][:].indirect(half_of(lst, c)), ACT.Sigmoid, bias=bias[:, t : t + 1], scale=slope[:, t : t + 1])
+            return dst
+
+        sg = [[], []]
+        sg2 = [[], []]
+        for t in range(PACK):
+            (nc.scalar.copy if t == 0 else nc.vector.tensor_copy)(y[t][:], y_bank[t][:])
+            sg[0].append(gate("sg", y, n1_l, sl_t, bias1, t, 0))
+
+        w3_bf = tile([P, N, PACK], BF16, "w3_bf", tag="w_bf")
+        for c in range(2):
+            gpsimd_round(w3_bf[:, cols(c), :], w3_raw[c][:].rearrange("p j c -> p c j"))
+        for t in range(PACK):
+            nc.vector.tensor_copy(d[t][:], d_bank[t][:])
+            sg2[0].append(gate("sg2_", d, n2_l, sl2_t, bias2, t, 0))
+
+        term1 = [tile([P, PACK, HALF], F32, f"term1_{c}") for c in range(2)]
+        term2 = [tile([P, PACK, HALF], F32, f"term2_{c}") for c in range(2)]
+        old = []
+        h_bank = [[psum.tile([P, HALF], F32, name=f"h_bank{c}{m}", tag=f"bank{PACK * c + m}") for m in range(PACK)] for c in range(2)]
+        sh = [[tile([P, HALF], F32, f"sh{c}{m}") for m in range(PACK)] for c in range(2)]
+        diff = [[tile([P, HALF], F32, f"diff{c}{m}") for m in range(PACK)] for c in range(2)]
+
+        def terms(dst, gates, vals, c):
+            for t in range(PACK):
+                nc.vector.scalar_tensor_tensor(dst[c][:, t, :], gates[c][t][:], gn_t[:, t : t + 1], vals[t][:, cols(c)], ALU.mult, ALU.mult)
+
+        def third_product(c):
+            z_bf = tile([P, HALF, PACK], BF16, f"z_bf{c}")
+            nc.vector.tensor_tensor(
+                z_bf[:].rearrange("p (c i) t -> p c t i", i=2),
+                term1[c][:].rearrange("p t (c i) -> p c t i", i=2),
+                term2[c][:].rearrange("p t (c i) -> p c t i", i=2),
+                ALU.add,
+            )
+            z_codes, z_plane = quantise(z_bf[:].rearrange("p j t -> p (j t)"), HALF, f"z{c}", 1)
+            for m in range(PACK):
+                project(w3_codes, w3_plane, m, z_codes[:], z_plane[:], h_bank[c][m][:])
+                nc.scalar.activation(sh[c][m][:], h_bank[c][m][:], ACT.Sigmoid)
+
+        def fetch_old(m):
+            old.append(tile([P, S], F32, f"old{m}", tag=f"d{m}"))
+            nc.scalar.activation(old[m][:], page[m][:].indirect(n3_l[:]), ACT.Copy)
+
+        def difference(c, m):
+            nc.vector.tensor_tensor(diff[c][m][:], h_bank[c][m][:], old[m][:, cols(c)], ALU.subtract)
+
+        def put(c, m, on_scalar):
+            step = tile([P, HALF], F32, f"step{c}{m}")
+            nc.vector.tensor_tensor(step[:], sh[c][m][:], diff[c][m][:], ALU.mult)
+            window = page[m][:].indirect(half_of(n3_l, c))
+            if on_scalar:
+                new = tile([P, HALF], F32, f"new{c}{m}")
+                nc.vector.tensor_tensor(new[:], step[:], old[m][:, cols(c)], ALU.add)
+                nc.scalar.activation(window, new[:], ACT.Copy)
+            else:
+                nc.vector.tensor_tensor(window, step[:], old[m][:, cols(c)], ALU.add)
+            if c == 1:
+                nc.sync.dma_start(out[m * P : (m + 1) * P, :], page[m][:])
+
+        terms(term1, sg, d, 0)
+        w3_codes, w3_plane = quantise(w3_bf[:].rearrange("p c j -> p (c j)"), N, "w3", 1)
+        terms(term2, sg2, y, 0)
+        for t in range(PACK):
+            sg[1].append(gate("sg", y, n1_l, sl_t, bias1, t, 1))
+        for t in range(PACK):
+            sg2[1].append(gate("sg2_", d, n2_l, sl2_t, bias2, t, 1))
+        third_product(0)
+        terms(term1, sg, d, 1)
+        terms(term2, sg2, y, 1)
+        for m in (0, 1, 2, 3):
+            fetch_old(m)
+        third_product(1)
+        for c in range(2):
+            if c == 0:
+                order = ((0, False), (2, True), (3, True), (1, False))
+            else:
+                order = ((2, True), (3, True), (0, False), (1, False))
+            for m, on_scalar in order:
+                difference(c, m)
+                put(c, m, on_scalar)

@@ -43,29 +43,32 @@ def tile_picked_twhcxbpaget_none_p_kernel(tc, x_words, x_scales, w1, w2, sl, th,
             return slice(c * HALF, (c + 1) * HALF)
 
         scale_win = tile([P, T], U8, "scale_win", tag="stage_a")
-        nc.gpsimd.memset(scale_win[:].bitcast(I32), 0)
-        for e in range(2):
-            nc.scalar.dma_start(scale_win[:].bitcast(I32)[e:P:16, :], x_scales[0].bitcast(I32)[e:16:2, :])
-        for e in range(2, 4):
-            nc.scalar.dma_start(scale_win[:].bitcast(I32)[e:P:32, :], x_scales[0].bitcast(I32)[e:16:4, :])
-
-        offs_l = load_list(offs, "offs_l")
-        hz_l = load_list(hz, "hz_l")
-
-        word_win = tile([P, T], I32, "word_win", tag="stage_b")
-        nc.sync.dma_start(word_win[:], x_words[0].rearrange("p n t -> p (n t)").bitcast(I32))
+        nc.vector.memset(scale_win[:].bitcast(I32), 0)
 
         def load_w_half(w, c, name, tag):
             raw = tile([P, PACK, HALF], F32, name, tag=tag)
             nc.sync.dma_start(raw[:], w.rearrange("(p j) c -> p j c", j=PACK)[:, :, cols(c)])
             return raw
 
-        w1_raw = [load_w_half(w1, c, f"w1_raw{c}", f"stage_c{c}") for c in range(2)]
+        offs_l = load_list(offs, "offs_l")
+        w1_raw = [load_w_half(w1, 0, "w1_raw0", "stage_c0")]
+        for e in range(2):
+            nc.sync.dma_start(scale_win[:].bitcast(I32)[e:P:16, :], x_scales[0].bitcast(I32)[e:16:2, :])
+        for e in range(2, 4):
+            nc.sync.dma_start(scale_win[:].bitcast(I32)[e:P:32, :], x_scales[0].bitcast(I32)[e:16:4, :])
+        hz_l = load_list(hz, "hz_l")
+        w1_raw.append(load_w_half(w1, 1, "w1_raw1", "stage_c1"))
+        word_win = tile([P, T], I32, "word_win", tag="stage_b")
+        nc.sync.dma_start(word_win[:], x_words[0].rearrange("p n t -> p (n t)").bitcast(I32))
         w2_raw = [load_w_half(w2, c, f"w2_raw{c}", f"stage_d{c}") for c in range(2)]
-
         n1_l = load_list(n1, "n1_l")
         n2_l = load_list(n2, "n2_l")
         n3_l = load_list(n3, "n3_l")
+
+        warm_in = tile([P, 1], F32, "warm_in")
+        warm_out = tile([P, 1], F32, "warm_out")
+        nc.gpsimd.memset(warm_in[:], 0.0)
+        nc.scalar.activation(warm_out[:], warm_in[:], ACT.Sigmoid)
 
         def load_rows(v, name):
             t = tile([P, PACK], F32, name)
@@ -80,21 +83,22 @@ def tile_picked_twhcxbpaget_none_p_kernel(tc, x_words, x_scales, w1, w2, sl, th,
 
         tok_plane = tile([P, S], U8, "tok_plane")
         hash_bytes = tile([P, S], U8, "hash_bytes")
-        hash_plane = tile([P, S], U8, "hash_plane")
+        x_tok = tile([P, S], U32, "x_tok")
+        nc.vector.tensor_copy(x_tok[:], word_win[:].bitcast(U32).indirect(offs_l[:]))
         nc.vector.tensor_copy(tok_plane[:], scale_win[:].indirect(offs_l[:]))
         nc.vector.tensor_copy(hash_bytes[:], scale_win[:].indirect(hz_l[:]))
+
+        hash_plane = tile([P, S], U8, "hash_plane")
         nc.vector.tensor_copy(hash_plane[:].bitcast(I32), hash_bytes[:].bitcast(I32))
         for e in range(2):
-            nc.gpsimd.dma_start(hash_plane[:].bitcast(I32)[2 + e : P : 32, :], hash_bytes[:].bitcast(I32)[16 + e : P : 32, :])
-        x_tok = tile([P, S], U32, "x_tok")
-        x_hash = tile([P, S], U32, "x_hash")
-        nc.vector.tensor_copy(x_tok[:], word_win[:].bitcast(U32).indirect(offs_l[:]))
-        nc.vector.tensor_copy(x_hash[:], word_win[:].bitcast(U32).indirect(hz_l[:]))
+            nc.sync.dma_start(hash_plane[:].bitcast(I32)[2 + e : P : 32, :], hash_bytes[:].bitcast(I32)[16 + e : P : 32, :])
 
         bias1 = tile([P, PACK], F32, "bias1")
         bias2 = tile([P, PACK], F32, "bias2")
-        nc.vector.scalar_tensor_tensor(bias1[:], sl_t[:], -1.0, th_t[:], ALU.mult, ALU.mult)
-        nc.vector.scalar_tensor_tensor(bias2[:], sl2_t[:], -1.0, th2_t[:], ALU.mult, ALU.mult)
+        for bias, slope, thr, name in ((bias1, sl_t, th_t, "prod1"), (bias2, sl2_t, th2_t, "prod2")):
+            prod = tile([P, PACK], F32, name)
+            nc.gpsimd.tensor_tensor(prod[:], slope[:], thr[:], ALU.mult)
+            nc.gpsimd.tensor_scalar(bias[:], prod[:], -1.0, 0.0, ALU.mult, ALU.add)
 
         def round_dealt(copy, grouped, raw, c):
             m = slice(c * HALF // PACK, (c + 1) * HALF // PACK)
@@ -121,6 +125,9 @@ def tile_picked_twhcxbpaget_none_p_kernel(tc, x_words, x_scales, w1, w2, sl, th,
         round_dealt(nc.scalar.copy, w1_bf, w1_raw[1], 1)
         w1_codes, w1_plane = quantise(w1_bf[:].rearrange("p t m j -> p (t m j)"), H, "w1", 2)
 
+        x_hash = tile([P, S], U32, "x_hash", tag="w1_bf")
+        nc.vector.tensor_copy(x_hash[:], word_win[:].bitcast(U32).indirect(hz_l[:]))
+
         y = [tile([P, S], F32, f"y{t}") for t in range(PACK)]
         d = [tile([P, S], F32, f"d{t}") for t in range(PACK)]
         y_bank = [psum.tile([P, S], F32, name=f"y_bank{t}", tag=f"bank{t}") for t in range(PACK)]
@@ -135,9 +142,9 @@ def tile_picked_twhcxbpaget_none_p_kernel(tc, x_words, x_scales, w1, w2, sl, th,
         for t in range(PACK):
             project(w2_codes, w2_plane, t, x_hash[:], hash_plane[:], d_bank[t][:])
 
-        w3_raw = [load_w_half(w3, 0, "w3_raw0", "stage_c0"), load_w_half(w3, 1, "w3_raw1", "stage_b")]
+        w3_raw = [load_w_half(w3, 0, "w3_raw0", "stage_c0"), load_w_half(w3, 1, "w3_raw1", "stage_c1")]
         page = []
-        for m, tag in enumerate(("stage_c1", "stage_a", "stage_d0", "stage_d1")):
+        for m, tag in enumerate(("stage_d0", "stage_d1", "stage_b", "x_tok")):
             pg = tile([P, U], F32, f"page{m}", tag=tag)
             nc.sync.dma_start(pg[:], mem[m * P : (m + 1) * P, :])
             page.append(pg)
@@ -150,7 +157,7 @@ def tile_picked_twhcxbpaget_none_p_kernel(tc, x_words, x_scales, w1, w2, sl, th,
         sg = [[], []]
         sg2 = [[], []]
         for t in range(PACK):
-            (nc.scalar.copy if t == 0 else nc.vector.tensor_copy)(y[t][:], y_bank[t][:])
+            (nc.scalar.copy if t < 2 else nc.vector.tensor_copy)(y[t][:], y_bank[t][:])
             sg[0].append(gate("sg", y, n1_l, sl_t, bias1, t, 0))
 
         w3_bf = tile([P, N, PACK], BF16, "w3_bf", tag="w_bf")
@@ -162,10 +169,9 @@ def tile_picked_twhcxbpaget_none_p_kernel(tc, x_words, x_scales, w1, w2, sl, th,
 
         term1 = [tile([P, PACK, HALF], F32, f"term1_{c}") for c in range(2)]
         term2 = [tile([P, PACK, HALF], F32, f"term2_{c}") for c in range(2)]
+        h_bank = [[psum.tile([P, 2, HALF], F32, name=f"h_bank{c}{g}", tag=f"bank{2 * c + g}") for g in range(2)] for c in range(2)]
+        sh = [[tile([P, 2, HALF], F32, f"sh{c}{g}") for g in range(2)] for c in range(2)]
         old = []
-        h_bank = [[psum.tile([P, HALF], F32, name=f"h_bank{c}{m}", tag=f"bank{PACK * c + m}") for m in range(PACK)] for c in range(2)]
-        sh = [[tile([P, HALF], F32, f"sh{c}{m}") for m in range(PACK)] for c in range(2)]
-        diff = [[tile([P, HALF], F32, f"diff{c}{m}") for m in range(PACK)] for c in range(2)]
 
         def terms(dst, gates, vals, c):
             for t in range(PACK):
@@ -180,20 +186,24 @@ def tile_picked_twhcxbpaget_none_p_kernel(tc, x_words, x_scales, w1, w2, sl, th,
                 ALU.add,
             )
             z_codes, z_plane = quantise(z_bf[:].rearrange("p j t -> p (j t)"), HALF, f"z{c}", 1)
-            for m in range(PACK):
-                project(w3_codes, w3_plane, m, z_codes[:], z_plane[:], h_bank[c][m][:])
-                nc.scalar.activation(sh[c][m][:], h_bank[c][m][:], ACT.Sigmoid)
+            for g in range(2):
+                for i in range(2):
+                    project(w3_codes, w3_plane, 2 * g + i, z_codes[:], z_plane[:], h_bank[c][g][:, i, :])
+                nc.scalar.activation(sh[c][g][:], h_bank[c][g][:], ACT.Sigmoid)
 
         def fetch_old(m):
-            old.append(tile([P, S], F32, f"old{m}", tag=f"d{m}"))
-            nc.scalar.activation(old[m][:], page[m][:].indirect(n3_l[:]), ACT.Copy)
+            old.append(old_all[:, m, :])
+            if m in ():
+                nc.vector.tensor_copy(old[m][:], page[m][:].indirect(n3_l[:]))
+            else:
+                nc.scalar.activation(old[m][:], page[m][:].indirect(n3_l[:]), ACT.Copy)
 
-        def difference(c, m):
-            nc.vector.tensor_tensor(diff[c][m][:], h_bank[c][m][:], old[m][:, cols(c)], ALU.subtract)
-
-        def put(c, m, on_scalar):
-            step = tile([P, HALF], F32, f"step{c}{m}")
-            nc.vector.tensor_tensor(step[:], sh[c][m][:], diff[c][m][:], ALU.mult)
+        def put(c, m, on_scalar, u):
+            g, i = divmod(m, 2)
+            diff = tile([P, HALF], F32, f"diff{c}{m}", tag=("term2_1", "z_bf1", "term1_1")[u % 2])
+            nc.vector.tensor_tensor(diff[:], h_bank[c][g][:, i, :], old[m][:, cols(c)], ALU.subtract)
+            step = tile([P, HALF], F32, f"step{c}{m}", tag=f"step{u % 2}")
+            nc.vector.tensor_tensor(step[:], sh[c][g][:, i, :], diff[:], ALU.mult)
             window = page[m][:].indirect(half_of(n3_l, c))
             if on_scalar:
                 new = tile([P, HALF], F32, f"new{c}{m}")
@@ -205,8 +215,8 @@ def tile_picked_twhcxbpaget_none_p_kernel(tc, x_words, x_scales, w1, w2, sl, th,
                 nc.sync.dma_start(out[m * P : (m + 1) * P, :], page[m][:])
 
         terms(term1, sg, d, 0)
-        w3_codes, w3_plane = quantise(w3_bf[:].rearrange("p c j -> p (c j)"), N, "w3", 1)
         terms(term2, sg2, y, 0)
+        w3_codes, w3_plane = quantise(w3_bf[:].rearrange("p c j -> p (c j)"), N, "w3", 1)
         for t in range(PACK):
             sg[1].append(gate("sg", y, n1_l, sl_t, bias1, t, 1))
         for t in range(PACK):
@@ -214,14 +224,9 @@ def tile_picked_twhcxbpaget_none_p_kernel(tc, x_words, x_scales, w1, w2, sl, th,
         third_product(0)
         terms(term1, sg, d, 1)
         terms(term2, sg2, y, 1)
-        for m in (0, 1, 2, 3):
+        old_all = tile([P, PACK, S], F32, "old_all", tag="z0_codes")
+        for m in range(PACK):
             fetch_old(m)
         third_product(1)
-        for c in range(2):
-            if c == 0:
-                order = ((0, False), (2, True), (3, True), (1, False))
-            else:
-                order = ((2, True), (3, True), (0, False), (1, False))
-            for m, on_scalar in order:
-                difference(c, m)
-                put(c, m, on_scalar)
+        for u, (c, m, on_scalar) in enumerate(((0, 0, False), (0, 1, True), (0, 2, True), (1, 1, True), (0, 3, False), (1, 2, True), (1, 3, True), (1, 0, False))):
+            put(c, m, on_scalar, u)

@@ -128,17 +128,22 @@ def tile_picked_twhcxbpaget_none_p_kernel(tc, x_words, x_scales, w1, w2, sl, th,
         x_hash = tile([P, S], U32, "x_hash", tag="w1_bf")
         nc.vector.tensor_copy(x_hash[:], word_win[:].bitcast(U32).indirect(hz_l[:]))
 
-        y = [tile([P, S], F32, f"y{t}") for t in range(PACK)]
+        y = []
         d = [tile([P, S], F32, f"d{t}") for t in range(PACK)]
         y_bank = [psum.tile([P, S], F32, name=f"y_bank{t}", tag=f"bank{t}") for t in range(PACK)]
         d_bank = [psum.tile([P, S], F32, name=f"d_bank{t}", tag=f"bank{PACK + t}") for t in range(PACK)]
         for t in range(PACK):
             project(w1_codes, w1_plane, t, x_tok[:], tok_plane[:], y_bank[t][:])
 
-        w2_bf = tile([P, PACK, P, PACK], BF16, "w2_bf", tag="w_bf")
-        round_dealt(nc.scalar.copy, w2_bf, w2_raw[0], 0)
-        round_dealt(nc.vector.tensor_copy, w2_bf, w2_raw[1], 1)
-        w2_codes, w2_plane = quantise(w2_bf[:].rearrange("p t m j -> p (t m j)"), H, "w2", 2)
+        w2_bf = [tile([P, 2, P, PACK], BF16, f"w2_bf{g}") for g in range(2)]
+        for c, copy in enumerate((nc.scalar.copy, nc.vector.tensor_copy)):
+            m = slice(c * HALF // PACK, (c + 1) * HALF // PACK)
+            for g in range(2):
+                copy(w2_bf[g][:, :, m, :].rearrange("p t m j -> p m j t"), w2_raw[c][:].rearrange("p j (m t) -> p m j t", t=PACK)[:, :, :, 2 * g : 2 * g + 2])
+        w2_codes = tile([P, H], U32, "w2_codes")
+        w2_plane = tile([P, H], U8, "w2_plane")
+        for g in range(2):
+            nc.vector.quantize_mx(w2_codes[:, cols(g)].bitcast(FP8X4), w2_plane[:, cols(g)], w2_bf[g][:].rearrange("p t m j -> p (t m j)"))
         for t in range(PACK):
             project(w2_codes, w2_plane, t, x_hash[:], hash_plane[:], d_bank[t][:])
 
@@ -157,10 +162,11 @@ def tile_picked_twhcxbpaget_none_p_kernel(tc, x_words, x_scales, w1, w2, sl, th,
         sg = [[], []]
         sg2 = [[], []]
         for t in range(PACK):
+            y.append(tile([P, S], F32, f"y{t}", tag="w2_bf0" if t == 2 else None))
             (nc.scalar.copy if t < 2 else nc.vector.tensor_copy)(y[t][:], y_bank[t][:])
             sg[0].append(gate("sg", y, n1_l, sl_t, bias1, t, 0))
 
-        w3_bf = tile([P, N, PACK], BF16, "w3_bf", tag="w_bf")
+        w3_bf = tile([P, N, PACK], BF16, "w3_bf", tag="w2_bf1")
         for c in range(2):
             gpsimd_round(w3_bf[:, cols(c), :], w3_raw[c][:].rearrange("p j c -> p c j"))
         for t in range(PACK):
@@ -169,7 +175,7 @@ def tile_picked_twhcxbpaget_none_p_kernel(tc, x_words, x_scales, w1, w2, sl, th,
 
         term1 = [tile([P, PACK, HALF], F32, f"term1_{c}") for c in range(2)]
         term2 = [tile([P, PACK, HALF], F32, f"term2_{c}") for c in range(2)]
-        h_bank = [[psum.tile([P, 2, HALF], F32, name=f"h_bank{c}{g}", tag=f"bank{2 * c + g}") for g in range(2)] for c in range(2)]
+        h_bank = []
         sh = [[tile([P, 2, HALF], F32, f"sh{c}{g}") for g in range(2)] for c in range(2)]
         old = []
 
@@ -186,14 +192,15 @@ def tile_picked_twhcxbpaget_none_p_kernel(tc, x_words, x_scales, w1, w2, sl, th,
                 ALU.add,
             )
             z_codes, z_plane = quantise(z_bf[:].rearrange("p j t -> p (j t)"), HALF, f"z{c}", 1)
+            h_bank.append([psum.tile([P, 2, HALF], F32, name=f"h_bank{c}{g}", tag=f"bank{2 * c + g}") for g in range(2)])
             for g in range(2):
                 for i in range(2):
                     project(w3_codes, w3_plane, 2 * g + i, z_codes[:], z_plane[:], h_bank[c][g][:, i, :])
                 nc.scalar.activation(sh[c][g][:], h_bank[c][g][:], ACT.Sigmoid)
 
         def fetch_old(m):
-            old.append(old_all[:, m, :])
-            if m in ():
+            old.append(old_v[:, m, :] if m < 1 else old_s[:, m - 1, :])
+            if m in (0,):
                 nc.vector.tensor_copy(old[m][:], page[m][:].indirect(n3_l[:]))
             else:
                 nc.scalar.activation(old[m][:], page[m][:].indirect(n3_l[:]), ACT.Copy)
@@ -212,21 +219,26 @@ def tile_picked_twhcxbpaget_none_p_kernel(tc, x_words, x_scales, w1, w2, sl, th,
             else:
                 nc.vector.tensor_tensor(window, step[:], old[m][:, cols(c)], ALU.add)
             if c == 1:
-                nc.sync.dma_start(out[m * P : (m + 1) * P, :], page[m][:])
+                (nc.scalar if m == 2 else nc.sync).dma_start(out[m * P : (m + 1) * P, :], page[m][:])
 
-        terms(term1, sg, d, 0)
-        terms(term2, sg2, y, 0)
+        y_gain = tile([P, PACK, HALF], F32, "y_gain", tag="stage_c1")
+        for t in range(PACK):
+            nc.gpsimd.tensor_scalar(y_gain[:, t, :], y[t][:, cols(1)], gn_t[:, t : t + 1], 0.0, ALU.mult, ALU.add)
+        terms(term1, sg, d_bank, 0)
+        terms(term2, sg2, y_bank, 0)
         w3_codes, w3_plane = quantise(w3_bf[:].rearrange("p c j -> p (c j)"), N, "w3", 1)
         for t in range(PACK):
             sg[1].append(gate("sg", y, n1_l, sl_t, bias1, t, 1))
         for t in range(PACK):
             sg2[1].append(gate("sg2_", d, n2_l, sl2_t, bias2, t, 1))
         third_product(0)
-        terms(term1, sg, d, 1)
-        terms(term2, sg2, y, 1)
-        old_all = tile([P, PACK, S], F32, "old_all", tag="z0_codes")
+        terms(term1, sg, d_bank, 1)
+        for t in range(PACK):
+            nc.gpsimd.tensor_tensor(term2[1][:, t, :], sg2[1][t][:], y_gain[:, t, :], ALU.mult)
+        old_v = tile([P, 1, S], F32, "old_v", tag="z_bf0")
+        old_s = tile([P, PACK - 1, S], F32, "old_s", tag="z0_codes")
         for m in range(PACK):
             fetch_old(m)
         third_product(1)
-        for u, (c, m, on_scalar) in enumerate(((0, 0, False), (0, 1, True), (0, 2, True), (1, 1, True), (0, 3, False), (1, 2, True), (1, 3, True), (1, 0, False))):
+        for u, (c, m, on_scalar) in enumerate(((0, 0, False), (0, 1, True), (0, 2, True), (0, 3, True), (1, 0, False), (1, 1, True), (1, 2, True), (1, 3, False))):
             put(c, m, on_scalar, u)

@@ -19,48 +19,61 @@ P = 128
 PACK = 4
 HALF = 256
 LIST_COLS = S // 16
+SCALE_ROWS = K // 32
+
+Y_TILES_ON_SCALAR = 2
+OLD_PAGES_ON_VECTOR = 2
+SCATTER_PAGES_ON_SCALAR = (3, 2)
 
 
-def tile_picked_twhcxbpaget_none_p_kernel(tc, x_words, x_scales, w1, w2, sl, th, sl2, th2, gn, w3, mem, offs, hz, n1, n2, n3, out):
+def tile_picked_twhcxbpaget_none_p_kernel(
+    tc, x_words, x_scales, w1, w2, sl, th, sl2, th2, gn, w3, mem, offs, hz, n1, n2, n3, out
+):
     nc = tc.nc
     with ExitStack() as ctx:
         lists = ctx.enter_context(tc.tile_pool(name="lists", bufs=1))
         sb = ctx.enter_context(tc.tile_pool(name="sb", bufs=1))
         psum = ctx.enter_context(tc.psum_pool(name="psum", bufs=1))
 
-        def tile(shape, dtype, name, tag=None):
-            return sb.tile(shape, dtype, name=name, tag=tag or name, align_bytes=64)
+        def tile(shape, dtype, name, reuse=None):
+            return sb.tile(shape, dtype, name=name, tag=reuse or name, align_bytes=64)
 
-        def load_list(src, name):
-            t = lists.tile([P, LIST_COLS], U16, name=name)
-            nc.sync.dma_start(t[:], src)
-            return t
-
-        def half_of(lst, c):
-            return lst[:, c * LIST_COLS // 2 : (c + 1) * LIST_COLS // 2]
-
-        def cols(c):
+        def half(c):
             return slice(c * HALF, (c + 1) * HALF)
 
-        scale_win = tile([P, T], U8, "scale_win", tag="stage_a")
-        nc.vector.memset(scale_win[:].bitcast(I32), 0)
+        def list_half(lst, c):
+            return lst[:, c * LIST_COLS // 2 : (c + 1) * LIST_COLS // 2]
 
-        def load_w_half(w, c, name, tag):
-            raw = tile([P, PACK, HALF], F32, name, tag=tag)
-            nc.sync.dma_start(raw[:], w.rearrange("(p j) c -> p j c", j=PACK)[:, :, cols(c)])
+        def load_list(src, name):
+            lst = lists.tile([P, LIST_COLS], U16, name=name)
+            nc.sync.dma_start(lst[:], src)
+            return lst
+
+        def load_weight_half(w, c, name, reuse=None):
+            raw = tile([P, PACK, HALF], F32, name, reuse)
+            nc.sync.dma_start(raw[:], w.rearrange("(p j) n -> p j n", j=PACK)[:, :, half(c)])
             return raw
 
+        def load_feature_values(v, name):
+            vals = tile([P, PACK], F32, name)
+            nc.gpsimd.dma_start(vals[:], v.rearrange("(p t) o -> p (t o)", t=PACK))
+            return vals
+
+        scale_win = tile([P, T], U8, "scale_win")
+        nc.vector.memset(scale_win[:].bitcast(I32), 0)
+        scale_rows = x_scales[0].bitcast(I32)
+
         offs_l = load_list(offs, "offs_l")
-        w1_raw = [load_w_half(w1, 0, "w1_raw0", "stage_c0")]
+        w1_raw = [load_weight_half(w1, 0, "w1_raw0")]
         for e in range(2):
-            nc.sync.dma_start(scale_win[:].bitcast(I32)[e:P:16, :], x_scales[0].bitcast(I32)[e:16:2, :])
-        for e in range(2, 4):
-            nc.sync.dma_start(scale_win[:].bitcast(I32)[e:P:32, :], x_scales[0].bitcast(I32)[e:16:4, :])
+            nc.sync.dma_start(scale_win[:].bitcast(I32)[e:P:16, :], scale_rows[e:SCALE_ROWS:2, :])
+        for r in range(2, 4):
+            nc.sync.dma_start(scale_win[:].bitcast(I32)[r:P:32, :], scale_rows[r:SCALE_ROWS:4, :])
         hz_l = load_list(hz, "hz_l")
-        w1_raw.append(load_w_half(w1, 1, "w1_raw1", "stage_c1"))
-        word_win = tile([P, T], I32, "word_win", tag="stage_b")
-        nc.sync.dma_start(word_win[:], x_words[0].rearrange("p n t -> p (n t)").bitcast(I32))
-        w2_raw = [load_w_half(w2, c, f"w2_raw{c}", f"stage_d{c}") for c in range(2)]
+        w1_raw.append(load_weight_half(w1, 1, "w1_raw1"))
+        word_win = tile([P, T], I32, "word_win")
+        nc.sync.dma_start(word_win[:], x_words[0].rearrange("p n j -> p (n j)").bitcast(I32))
+        w2_raw = [load_weight_half(w2, c, f"w2_raw{c}") for c in range(2)]
         n1_l = load_list(n1, "n1_l")
         n2_l = load_list(n2, "n2_l")
         n3_l = load_list(n3, "n3_l")
@@ -70,21 +83,16 @@ def tile_picked_twhcxbpaget_none_p_kernel(tc, x_words, x_scales, w1, w2, sl, th,
         nc.gpsimd.memset(warm_in[:], 0.0)
         nc.scalar.activation(warm_out[:], warm_in[:], ACT.Sigmoid)
 
-        def load_rows(v, name):
-            t = tile([P, PACK], F32, name)
-            nc.gpsimd.dma_start(t[:], v.rearrange("(p t) o -> p (t o)", t=PACK))
-            return t
-
-        sl_t = load_rows(sl, "sl_t")
-        th_t = load_rows(th, "th_t")
-        sl2_t = load_rows(sl2, "sl2_t")
-        th2_t = load_rows(th2, "th2_t")
-        gn_t = load_rows(gn, "gn_t")
+        slope1 = load_feature_values(sl, "slope1")
+        thresh1 = load_feature_values(th, "thresh1")
+        slope2 = load_feature_values(sl2, "slope2")
+        thresh2 = load_feature_values(th2, "thresh2")
+        gain = load_feature_values(gn, "gain")
 
         tok_plane = tile([P, S], U8, "tok_plane")
         hash_bytes = tile([P, S], U8, "hash_bytes")
-        x_tok = tile([P, S], U32, "x_tok")
-        nc.vector.tensor_copy(x_tok[:], word_win[:].bitcast(U32).indirect(offs_l[:]))
+        tok_words = tile([P, S], U32, "tok_words")
+        nc.vector.tensor_copy(tok_words[:], word_win[:].bitcast(U32).indirect(offs_l[:]))
         nc.vector.tensor_copy(tok_plane[:], scale_win[:].indirect(offs_l[:]))
         nc.vector.tensor_copy(hash_bytes[:], scale_win[:].indirect(hz_l[:]))
 
@@ -95,150 +103,160 @@ def tile_picked_twhcxbpaget_none_p_kernel(tc, x_words, x_scales, w1, w2, sl, th,
 
         bias1 = tile([P, PACK], F32, "bias1")
         bias2 = tile([P, PACK], F32, "bias2")
-        for bias, slope, thr, name in ((bias1, sl_t, th_t, "prod1"), (bias2, sl2_t, th2_t, "prod2")):
+        for bias, slope, thresh, name in ((bias1, slope1, thresh1, "prod1"), (bias2, slope2, thresh2, "prod2")):
             prod = tile([P, PACK], F32, name)
-            nc.gpsimd.tensor_tensor(prod[:], slope[:], thr[:], ALU.mult)
+            nc.gpsimd.tensor_tensor(prod[:], slope[:], thresh[:], ALU.mult)
             nc.gpsimd.tensor_scalar(bias[:], prod[:], -1.0, 0.0, ALU.mult, ALU.add)
 
-        def round_dealt(copy, grouped, raw, c):
-            m = slice(c * HALF // PACK, (c + 1) * HALF // PACK)
-            copy(grouped[:, :, m, :].rearrange("p t m j -> p m j t"), raw[:].rearrange("p j (m t) -> p m j t", t=PACK))
+        def round_dealt(copy, grouped, raw, c, t0):
+            tiles = grouped.shape[1]
+            f = slice(c * HALF // PACK, (c + 1) * HALF // PACK)
+            copy(
+                grouped[:, :, f, :].rearrange("p t f j -> p f j t"),
+                raw[:].rearrange("p j (f t) -> p f j t", t=PACK)[:, :, :, t0 : t0 + tiles],
+            )
 
-        def gpsimd_round(dst, src):
-            nc.gpsimd.tensor_scalar(dst, src, 1.0, 0.0, ALU.mult, ALU.add)
-
-        def quantise(grouped_flat, width, name, pieces):
-            codes = tile([P, width], U32, name + "_codes")
-            plane = tile([P, width], U8, name + "_plane")
-            step = width // pieces
-            for i in range(pieces):
-                s = slice(i * step, (i + 1) * step)
-                nc.vector.quantize_mx(codes[:, s].bitcast(FP8X4), plane[:, s], grouped_flat[:, PACK * i * step : PACK * (i + 1) * step])
+        def quantise(pieces, name):
+            n = pieces[0].shape[1] // PACK
+            codes = tile([P, n * len(pieces)], U32, name + "_codes")
+            plane = tile([P, n * len(pieces)], U8, name + "_plane")
+            for i, piece in enumerate(pieces):
+                nc.vector.quantize_mx(codes[:, i * n : (i + 1) * n].bitcast(FP8X4), plane[:, i * n : (i + 1) * n], piece)
             return codes, plane
 
-        def project(codes, plane, t, x, x_scale, bank):
-            m = slice(t * P, (t + 1) * P)
-            nc.tensor.matmul_mx(bank, lhsT=codes[:, m].bitcast(FP8X4), lhsT_scale=plane[:, m], rhs=x.bitcast(FP8X4), rhs_scale=x_scale, start=True, stop=True)
+        def product(weights, i, words, plane, bank):
+            w_codes, w_plane = weights
+            w_cols = slice(i * P, (i + 1) * P)
+            nc.tensor.matmul_mx(
+                bank,
+                lhsT=w_codes[:, w_cols].bitcast(FP8X4),
+                lhsT_scale=w_plane[:, w_cols],
+                rhs=words.bitcast(FP8X4),
+                rhs_scale=plane,
+                start=True,
+                stop=True,
+            )
 
         w1_bf = tile([P, PACK, P, PACK], BF16, "w1_bf")
-        round_dealt(nc.scalar.copy, w1_bf, w1_raw[0], 0)
-        round_dealt(nc.scalar.copy, w1_bf, w1_raw[1], 1)
-        w1_codes, w1_plane = quantise(w1_bf[:].rearrange("p t m j -> p (t m j)"), H, "w1", 2)
+        for c in range(2):
+            round_dealt(nc.scalar.copy, w1_bf, w1_raw[c], c, 0)
+        w1_q = quantise([w1_bf[:, 2 * g : 2 * g + 2].rearrange("p t f j -> p (t f j)") for g in range(2)], "w1")
 
-        x_hash = tile([P, S], U32, "x_hash", tag="w1_bf")
-        nc.vector.tensor_copy(x_hash[:], word_win[:].bitcast(U32).indirect(hz_l[:]))
+        hash_words = tile([P, S], U32, "hash_words", reuse="w1_bf")
+        nc.vector.tensor_copy(hash_words[:], word_win[:].bitcast(U32).indirect(hz_l[:]))
 
-        y = []
         d = [tile([P, S], F32, f"d{t}") for t in range(PACK)]
         y_bank = [psum.tile([P, S], F32, name=f"y_bank{t}", tag=f"bank{t}") for t in range(PACK)]
         d_bank = [psum.tile([P, S], F32, name=f"d_bank{t}", tag=f"bank{PACK + t}") for t in range(PACK)]
         for t in range(PACK):
-            project(w1_codes, w1_plane, t, x_tok[:], tok_plane[:], y_bank[t][:])
+            product(w1_q, t, tok_words[:], tok_plane[:], y_bank[t][:])
 
         w2_bf = [tile([P, 2, P, PACK], BF16, f"w2_bf{g}") for g in range(2)]
         for c, copy in enumerate((nc.scalar.copy, nc.vector.tensor_copy)):
-            m = slice(c * HALF // PACK, (c + 1) * HALF // PACK)
             for g in range(2):
-                copy(w2_bf[g][:, :, m, :].rearrange("p t m j -> p m j t"), w2_raw[c][:].rearrange("p j (m t) -> p m j t", t=PACK)[:, :, :, 2 * g : 2 * g + 2])
-        w2_codes = tile([P, H], U32, "w2_codes")
-        w2_plane = tile([P, H], U8, "w2_plane")
-        for g in range(2):
-            nc.vector.quantize_mx(w2_codes[:, cols(g)].bitcast(FP8X4), w2_plane[:, cols(g)], w2_bf[g][:].rearrange("p t m j -> p (t m j)"))
+                round_dealt(copy, w2_bf[g], w2_raw[c], c, 2 * g)
+        w2_q = quantise([w2_bf[g][:].rearrange("p t f j -> p (t f j)") for g in range(2)], "w2")
         for t in range(PACK):
-            project(w2_codes, w2_plane, t, x_hash[:], hash_plane[:], d_bank[t][:])
+            product(w2_q, t, hash_words[:], hash_plane[:], d_bank[t][:])
 
-        w3_raw = [load_w_half(w3, 0, "w3_raw0", "stage_c0"), load_w_half(w3, 1, "w3_raw1", "stage_c1")]
+        w3_raw = [load_weight_half(w3, c, f"w3_raw{c}", reuse=f"w1_raw{c}") for c in range(2)]
         page = []
-        for m, tag in enumerate(("stage_d0", "stage_d1", "stage_b", "x_tok")):
-            pg = tile([P, U], F32, f"page{m}", tag=tag)
-            nc.sync.dma_start(pg[:], mem[m * P : (m + 1) * P, :])
-            page.append(pg)
+        for m, spent in enumerate(("w2_raw0", "w2_raw1", "word_win", "tok_words")):
+            page.append(tile([P, U], F32, f"page{m}", reuse=spent))
+            nc.sync.dma_start(page[m][:], mem[m * P : (m + 1) * P, :])
 
-        def gate(name, src, lst, slope, bias, t, c):
-            dst = tile([P, HALF], F32, f"{name}{c}{t}", tag=f"{name}{t}")
-            nc.scalar.activation(dst[:], src[t][:].indirect(half_of(lst, c)), ACT.Sigmoid, bias=bias[:, t : t + 1], scale=slope[:, t : t + 1])
-            return dst
+        def gate(name, rows, lst, slope, bias, t, c):
+            res = tile([P, HALF], F32, f"{name}{c}{t}", reuse=f"{name}{t}")
+            nc.scalar.activation(
+                res[:], rows[t][:].indirect(list_half(lst, c)), ACT.Sigmoid, bias=bias[:, t : t + 1], scale=slope[:, t : t + 1]
+            )
+            return res
 
+        y = []
         sg = [[], []]
         sg2 = [[], []]
         for t in range(PACK):
-            y.append(tile([P, S], F32, f"y{t}", tag="w2_bf0" if t == 2 else None))
-            (nc.scalar.copy if t < 2 else nc.vector.tensor_copy)(y[t][:], y_bank[t][:])
-            sg[0].append(gate("sg", y, n1_l, sl_t, bias1, t, 0))
+            y.append(tile([P, S], F32, f"y{t}", reuse="w2_bf0" if t == Y_TILES_ON_SCALAR else None))
+            copy = nc.scalar.copy if t < Y_TILES_ON_SCALAR else nc.vector.tensor_copy
+            copy(y[t][:], y_bank[t][:])
+            sg[0].append(gate("sg", y, n1_l, slope1, bias1, t, 0))
 
-        w3_bf = tile([P, N, PACK], BF16, "w3_bf", tag="w2_bf1")
+        w3_bf = tile([P, N, PACK], BF16, "w3_bf", reuse="w2_bf1")
         for c in range(2):
-            gpsimd_round(w3_bf[:, cols(c), :], w3_raw[c][:].rearrange("p j c -> p c j"))
+            nc.gpsimd.tensor_scalar(w3_bf[:, half(c), :], w3_raw[c][:].rearrange("p j n -> p n j"), 1.0, 0.0, ALU.mult, ALU.add)
         for t in range(PACK):
             nc.vector.tensor_copy(d[t][:], d_bank[t][:])
-            sg2[0].append(gate("sg2_", d, n2_l, sl2_t, bias2, t, 0))
+            sg2[0].append(gate("sg2_", d, n2_l, slope2, bias2, t, 0))
 
         term1 = [tile([P, PACK, HALF], F32, f"term1_{c}") for c in range(2)]
         term2 = [tile([P, PACK, HALF], F32, f"term2_{c}") for c in range(2)]
         h_bank = []
-        sh = [[tile([P, 2, HALF], F32, f"sh{c}{g}") for g in range(2)] for c in range(2)]
-        old = []
+        sig_h = [[tile([P, 2, HALF], F32, f"sig_h{c}{g}") for g in range(2)] for c in range(2)]
 
-        def terms(dst, gates, vals, c):
+        def vector_terms(term, gates, banks, c):
             for t in range(PACK):
-                nc.vector.scalar_tensor_tensor(dst[c][:, t, :], gates[c][t][:], gn_t[:, t : t + 1], vals[t][:, cols(c)], ALU.mult, ALU.mult)
+                nc.vector.scalar_tensor_tensor(
+                    term[c][:, t, :], gates[c][t][:], gain[:, t : t + 1], banks[t][:, half(c)], ALU.mult, ALU.mult
+                )
 
         def third_product(c):
             z_bf = tile([P, HALF, PACK], BF16, f"z_bf{c}")
             nc.vector.tensor_tensor(
-                z_bf[:].rearrange("p (c i) t -> p c t i", i=2),
-                term1[c][:].rearrange("p t (c i) -> p c t i", i=2),
-                term2[c][:].rearrange("p t (c i) -> p c t i", i=2),
+                z_bf[:].rearrange("p (n i) t -> p n t i", i=2),
+                term1[c][:].rearrange("p t (n i) -> p n t i", i=2),
+                term2[c][:].rearrange("p t (n i) -> p n t i", i=2),
                 ALU.add,
             )
-            z_codes, z_plane = quantise(z_bf[:].rearrange("p j t -> p (j t)"), HALF, f"z{c}", 1)
+            z_codes, z_plane = quantise([z_bf[:].rearrange("p n t -> p (n t)")], f"z{c}")
             h_bank.append([psum.tile([P, 2, HALF], F32, name=f"h_bank{c}{g}", tag=f"bank{2 * c + g}") for g in range(2)])
             for g in range(2):
                 for i in range(2):
-                    project(w3_codes, w3_plane, 2 * g + i, z_codes[:], z_plane[:], h_bank[c][g][:, i, :])
-                nc.scalar.activation(sh[c][g][:], h_bank[c][g][:], ACT.Sigmoid)
+                    product(w3_q, 2 * g + i, z_codes[:], z_plane[:], h_bank[c][g][:, i, :])
+                nc.scalar.activation(sig_h[c][g][:], h_bank[c][g][:], ACT.Sigmoid)
 
-        def fetch_old(m):
-            old.append(old_v[:, m, :] if m < 1 else old_s[:, m - 1, :])
-            if m in (0,):
-                nc.vector.tensor_copy(old[m][:], page[m][:].indirect(n3_l[:]))
-            else:
-                nc.scalar.activation(old[m][:], page[m][:].indirect(n3_l[:]), ACT.Copy)
-
-        def put(c, m, on_scalar, u):
-            g, i = divmod(m, 2)
-            diff = tile([P, HALF], F32, f"diff{c}{m}", tag=("term2_1", "z_bf1", "term1_1")[u % 2])
-            nc.vector.tensor_tensor(diff[:], h_bank[c][g][:, i, :], old[m][:, cols(c)], ALU.subtract)
-            step = tile([P, HALF], F32, f"step{c}{m}", tag=f"step{u % 2}")
-            nc.vector.tensor_tensor(step[:], sh[c][g][:, i, :], diff[:], ALU.mult)
-            window = page[m][:].indirect(half_of(n3_l, c))
-            if on_scalar:
-                new = tile([P, HALF], F32, f"new{c}{m}")
-                nc.vector.tensor_tensor(new[:], step[:], old[m][:, cols(c)], ALU.add)
-                nc.scalar.activation(window, new[:], ACT.Copy)
-            else:
-                nc.vector.tensor_tensor(window, step[:], old[m][:, cols(c)], ALU.add)
-            if c == 1:
-                (nc.scalar if m == 2 else nc.sync).dma_start(out[m * P : (m + 1) * P, :], page[m][:])
-
-        y_gain = tile([P, PACK, HALF], F32, "y_gain", tag="stage_c1")
+        y_gain = tile([P, PACK, HALF], F32, "y_gain", reuse="w1_raw1")
         for t in range(PACK):
-            nc.gpsimd.tensor_scalar(y_gain[:, t, :], y[t][:, cols(1)], gn_t[:, t : t + 1], 0.0, ALU.mult, ALU.add)
-        terms(term1, sg, d_bank, 0)
-        terms(term2, sg2, y_bank, 0)
-        w3_codes, w3_plane = quantise(w3_bf[:].rearrange("p c j -> p (c j)"), N, "w3", 1)
+            nc.gpsimd.tensor_scalar(y_gain[:, t, :], y[t][:, half(1)], gain[:, t : t + 1], 0.0, ALU.mult, ALU.add)
+        vector_terms(term1, sg, d_bank, 0)
+        vector_terms(term2, sg2, y_bank, 0)
+        w3_q = quantise([w3_bf[:].rearrange("p n j -> p (n j)")], "w3")
         for t in range(PACK):
-            sg[1].append(gate("sg", y, n1_l, sl_t, bias1, t, 1))
+            sg[1].append(gate("sg", y, n1_l, slope1, bias1, t, 1))
         for t in range(PACK):
-            sg2[1].append(gate("sg2_", d, n2_l, sl2_t, bias2, t, 1))
+            sg2[1].append(gate("sg2_", d, n2_l, slope2, bias2, t, 1))
         third_product(0)
-        terms(term1, sg, d_bank, 1)
+        vector_terms(term1, sg, d_bank, 1)
         for t in range(PACK):
             nc.gpsimd.tensor_tensor(term2[1][:, t, :], sg2[1][t][:], y_gain[:, t, :], ALU.mult)
-        old_v = tile([P, 1, S], F32, "old_v", tag="z_bf0")
-        old_s = tile([P, PACK - 1, S], F32, "old_s", tag="z0_codes")
+
+        old_by_vector = tile([P, OLD_PAGES_ON_VECTOR, S], F32, "old_by_vector", reuse="z_bf0")
+        old_by_scalar = tile([P, PACK - OLD_PAGES_ON_VECTOR, S], F32, "old_by_scalar", reuse="z0_codes")
+        old = []
         for m in range(PACK):
-            fetch_old(m)
+            slots = page[m][:].indirect(n3_l[:])
+            if m < OLD_PAGES_ON_VECTOR:
+                old.append(old_by_vector[:, m, :])
+                nc.vector.tensor_copy(old[m], slots)
+            else:
+                old.append(old_by_scalar[:, m - OLD_PAGES_ON_VECTOR, :])
+                nc.scalar.activation(old[m], slots, ACT.Copy)
         third_product(1)
-        for u, (c, m, on_scalar) in enumerate(((0, 0, False), (0, 1, True), (0, 2, True), (0, 3, True), (1, 0, False), (1, 1, True), (1, 2, True), (1, 3, False))):
-            put(c, m, on_scalar, u)
+
+        for c in range(2):
+            for m in range(PACK):
+                g, i = divmod(m, 2)
+                old_half = old[m][:, half(c)]
+                diff = tile([P, HALF], F32, f"diff{c}{m}", reuse=("term2_0", "term1_0")[i])
+                nc.vector.tensor_tensor(diff[:], h_bank[c][g][:, i, :], old_half, ALU.subtract)
+                step = tile([P, HALF], F32, f"step{c}{m}", reuse=f"step{i}")
+                nc.vector.tensor_tensor(step[:], sig_h[c][g][:, i, :], diff[:], ALU.mult)
+                slots = page[m][:].indirect(list_half(n3_l, c))
+                if m < SCATTER_PAGES_ON_SCALAR[c]:
+                    new = tile([P, HALF], F32, f"new{c}{m}")
+                    nc.vector.tensor_tensor(new[:], step[:], old_half, ALU.add)
+                    nc.scalar.activation(slots, new[:], ACT.Copy)
+                else:
+                    nc.vector.tensor_tensor(slots, step[:], old_half, ALU.add)
+                if c == 1:
+                    queue = nc.scalar if m == SCATTER_PAGES_ON_SCALAR[c] - 1 else nc.sync
+                    queue.dma_start(out[m * P : (m + 1) * P, :], page[m][:])

from contextlib import ExitStack

import concourse.mybir as mybir

K, T, S, N, H, U = 512, 2048, 512, 512, 512, 1024
FLOPS = 2 * S * (2 * K * H + H * N)

F32 = mybir.dt.float32
BF16 = mybir.dt.bfloat16
I32 = mybir.dt.int32
U32 = mybir.dt.uint32
U16 = mybir.dt.uint16
U8 = mybir.dt.uint8
FP8X4 = mybir.dt.float8_e4m3fn_x4
ALU = mybir.AluOpType
ACT = mybir.ActivationFunctionType

P = 128
PACK = 4
HALF = 256
LIST_COLS = S // 16
SCALE_ROWS = K // 32

Y_TILES_ON_SCALAR = 2
OLD_PAGES_ON_VECTOR = 2
SCATTER_PAGES_ON_SCALAR = (3, 2)


def tile_picked_twhcxbpaget_none_p_kernel(
    tc, x_words, x_scales, w1, w2, sl, th, sl2, th2, gn, w3, mem, offs, hz, n1, n2, n3, out
):
    nc = tc.nc
    with ExitStack() as ctx:
        lists = ctx.enter_context(tc.tile_pool(name="lists", bufs=1))
        sb = ctx.enter_context(tc.tile_pool(name="sb", bufs=1))
        psum = ctx.enter_context(tc.psum_pool(name="psum", bufs=1))

        def tile(shape, dtype, name, reuse=None):
            return sb.tile(shape, dtype, name=name, tag=reuse or name, align_bytes=64)

        def half(c):
            return slice(c * HALF, (c + 1) * HALF)

        def list_half(lst, c):
            return lst[:, c * LIST_COLS // 2 : (c + 1) * LIST_COLS // 2]

        def load_list(src, name):
            lst = lists.tile([P, LIST_COLS], U16, name=name)
            nc.sync.dma_start(lst[:], src)
            return lst

        def load_weight_half(w, c, name, reuse=None):
            raw = tile([P, PACK, HALF], F32, name, reuse)
            nc.sync.dma_start(raw[:], w.rearrange("(p j) n -> p j n", j=PACK)[:, :, half(c)])
            return raw

        def load_feature_values(v, name):
            vals = tile([P, PACK], F32, name)
            nc.gpsimd.dma_start(vals[:], v.rearrange("(p t) o -> p (t o)", t=PACK))
            return vals

        scale_win = tile([P, T], U8, "scale_win")
        nc.vector.memset(scale_win[:].bitcast(I32), 0)
        scale_rows = x_scales[0].bitcast(I32)

        offs_l = load_list(offs, "offs_l")
        w1_raw = [load_weight_half(w1, 0, "w1_raw0")]
        for e in range(2):
            nc.sync.dma_start(scale_win[:].bitcast(I32)[e:P:16, :], scale_rows[e:SCALE_ROWS:2, :])
        for r in range(2, 4):
            nc.sync.dma_start(scale_win[:].bitcast(I32)[r:P:32, :], scale_rows[r:SCALE_ROWS:4, :])
        hz_l = load_list(hz, "hz_l")
        w1_raw.append(load_weight_half(w1, 1, "w1_raw1"))
        word_win = tile([P, T], I32, "word_win")
        nc.sync.dma_start(word_win[:], x_words[0].rearrange("p n j -> p (n j)").bitcast(I32))
        w2_raw = [load_weight_half(w2, c, f"w2_raw{c}") for c in range(2)]
        n1_l = load_list(n1, "n1_l")
        n2_l = load_list(n2, "n2_l")
        n3_l = load_list(n3, "n3_l")

        warm_in = tile([P, 1], F32, "warm_in")
        warm_out = tile([P, 1], F32, "warm_out")
        nc.gpsimd.memset(warm_in[:], 0.0)
        nc.scalar.activation(warm_out[:], warm_in[:], ACT.Sigmoid)

        slope1 = load_feature_values(sl, "slope1")
        thresh1 = load_feature_values(th, "thresh1")
        slope2 = load_feature_values(sl2, "slope2")
        thresh2 = load_feature_values(th2, "thresh2")
        gain = load_feature_values(gn, "gain")

        tok_plane = tile([P, S], U8, "tok_plane")
        hash_bytes = tile([P, S], U8, "hash_bytes")
        tok_words = tile([P, S], U32, "tok_words")
        nc.vector.tensor_copy(tok_words[:], word_win[:].bitcast(U32).indirect(offs_l[:]))
        nc.vector.tensor_copy(tok_plane[:], scale_win[:].indirect(offs_l[:]))
        nc.vector.tensor_copy(hash_bytes[:], scale_win[:].indirect(hz_l[:]))

        hash_plane = tile([P, S], U8, "hash_plane")
        nc.vector.tensor_copy(hash_plane[:].bitcast(I32), hash_bytes[:].bitcast(I32))
        for e in range(2):
            nc.sync.dma_start(hash_plane[:].bitcast(I32)[2 + e : P : 32, :], hash_bytes[:].bitcast(I32)[16 + e : P : 32, :])

        bias1 = tile([P, PACK], F32, "bias1")
        bias2 = tile([P, PACK], F32, "bias2")
        for bias, slope, thresh, name in ((bias1, slope1, thresh1, "prod1"), (bias2, slope2, thresh2, "prod2")):
            prod = tile([P, PACK], F32, name)
            nc.gpsimd.tensor_tensor(prod[:], slope[:], thresh[:], ALU.mult)
            nc.gpsimd.tensor_scalar(bias[:], prod[:], -1.0, 0.0, ALU.mult, ALU.add)

        def round_dealt(copy, grouped, raw, c, t0):
            tiles = grouped.shape[1]
            f = slice(c * HALF // PACK, (c + 1) * HALF // PACK)
            copy(
                grouped[:, :, f, :].rearrange("p t f j -> p f j t"),
                raw[:].rearrange("p j (f t) -> p f j t", t=PACK)[:, :, :, t0 : t0 + tiles],
            )

        def quantise(pieces, name):
            n = pieces[0].shape[1] // PACK
            codes = tile([P, n * len(pieces)], U32, name + "_codes")
            plane = tile([P, n * len(pieces)], U8, name + "_plane")
            for i, piece in enumerate(pieces):
                nc.vector.quantize_mx(codes[:, i * n : (i + 1) * n].bitcast(FP8X4), plane[:, i * n : (i + 1) * n], piece)
            return codes, plane

        def product(weights, i, words, plane, bank):
            w_codes, w_plane = weights
            w_cols = slice(i * P, (i + 1) * P)
            nc.tensor.matmul_mx(
                bank,
                lhsT=w_codes[:, w_cols].bitcast(FP8X4),
                lhsT_scale=w_plane[:, w_cols],
                rhs=words.bitcast(FP8X4),
                rhs_scale=plane,
                start=True,
                stop=True,
            )

        w1_bf = tile([P, PACK, P, PACK], BF16, "w1_bf")
        for c in range(2):
            round_dealt(nc.scalar.copy, w1_bf, w1_raw[c], c, 0)
        w1_q = quantise([w1_bf[:, 2 * g : 2 * g + 2].rearrange("p t f j -> p (t f j)") for g in range(2)], "w1")

        hash_words = tile([P, S], U32, "hash_words", reuse="w1_bf")
        nc.vector.tensor_copy(hash_words[:], word_win[:].bitcast(U32).indirect(hz_l[:]))

        d = [tile([P, S], F32, f"d{t}") for t in range(PACK)]
        y_bank = [psum.tile([P, S], F32, name=f"y_bank{t}", tag=f"bank{t}") for t in range(PACK)]
        d_bank = [psum.tile([P, S], F32, name=f"d_bank{t}", tag=f"bank{PACK + t}") for t in range(PACK)]
        for t in range(PACK):
            product(w1_q, t, tok_words[:], tok_plane[:], y_bank[t][:])

        w2_bf = [tile([P, 2, P, PACK], BF16, f"w2_bf{g}") for g in range(2)]
        for c, copy in enumerate((nc.scalar.copy, nc.vector.tensor_copy)):
            for g in range(2):
                round_dealt(copy, w2_bf[g], w2_raw[c], c, 2 * g)
        w2_q = quantise([w2_bf[g][:].rearrange("p t f j -> p (t f j)") for g in range(2)], "w2")
        for t in range(PACK):
            product(w2_q, t, hash_words[:], hash_plane[:], d_bank[t][:])

        w3_raw = [load_weight_half(w3, c, f"w3_raw{c}", reuse=f"w1_raw{c}") for c in range(2)]
        page = []
        for m, spent in enumerate(("w2_raw0", "w2_raw1", "word_win", "tok_words")):
            page.append(tile([P, U], F32, f"page{m}", reuse=spent))
            nc.sync.dma_start(page[m][:], mem[m * P : (m + 1) * P, :])

        def gate(name, rows, lst, slope, bias, t, c):
            res = tile([P, HALF], F32, f"{name}{c}{t}", reuse=f"{name}{t}")
            nc.scalar.activation(
                res[:], rows[t][:].indirect(list_half(lst, c)), ACT.Sigmoid, bias=bias[:, t : t + 1], scale=slope[:, t : t + 1]
            )
            return res

        y = []
        sg = [[], []]
        sg2 = [[], []]
        for t in range(PACK):
            y.append(tile([P, S], F32, f"y{t}", reuse="w2_bf0" if t == Y_TILES_ON_SCALAR else None))
            copy = nc.scalar.copy if t < Y_TILES_ON_SCALAR else nc.vector.tensor_copy
            copy(y[t][:], y_bank[t][:])
            sg[0].append(gate("sg", y, n1_l, slope1, bias1, t, 0))

        w3_bf = tile([P, N, PACK], BF16, "w3_bf", reuse="w2_bf1")
        for c in range(2):
            nc.gpsimd.tensor_scalar(w3_bf[:, half(c), :], w3_raw[c][:].rearrange("p j n -> p n j"), 1.0, 0.0, ALU.mult, ALU.add)
        for t in range(PACK):
            nc.vector.tensor_copy(d[t][:], d_bank[t][:])
            sg2[0].append(gate("sg2_", d, n2_l, slope2, bias2, t, 0))

        term1 = [tile([P, PACK, HALF], F32, f"term1_{c}") for c in range(2)]
        term2 = [tile([P, PACK, HALF], F32, f"term2_{c}") for c in range(2)]
        h_bank = []
        sig_h = [[tile([P, 2, HALF], F32, f"sig_h{c}{g}") for g in range(2)] for c in range(2)]

        def vector_terms(term, gates, banks, c):
            for t in range(PACK):
                nc.vector.scalar_tensor_tensor(
                    term[c][:, t, :], gates[c][t][:], gain[:, t : t + 1], banks[t][:, half(c)], ALU.mult, ALU.mult
                )

        def third_product(c):
            z_bf = tile([P, HALF, PACK], BF16, f"z_bf{c}")
            nc.vector.tensor_tensor(
                z_bf[:].rearrange("p (n i) t -> p n t i", i=2),
                term1[c][:].rearrange("p t (n i) -> p n t i", i=2),
                term2[c][:].rearrange("p t (n i) -> p n t i", i=2),
                ALU.add,
            )
            z_codes, z_plane = quantise([z_bf[:].rearrange("p n t -> p (n t)")], f"z{c}")
            h_bank.append([psum.tile([P, 2, HALF], F32, name=f"h_bank{c}{g}", tag=f"bank{2 * c + g}") for g in range(2)])
            for g in range(2):
                for i in range(2):
                    product(w3_q, 2 * g + i, z_codes[:], z_plane[:], h_bank[c][g][:, i, :])
                nc.scalar.activation(sig_h[c][g][:], h_bank[c][g][:], ACT.Sigmoid)

        y_gain = tile([P, PACK, HALF], F32, "y_gain", reuse="w1_raw1")
        for t in range(PACK):
            nc.gpsimd.tensor_scalar(y_gain[:, t, :], y[t][:, half(1)], gain[:, t : t + 1], 0.0, ALU.mult, ALU.add)
        vector_terms(term1, sg, d_bank, 0)
        vector_terms(term2, sg2, y_bank, 0)
        w3_q = quantise([w3_bf[:].rearrange("p n j -> p (n j)")], "w3")
        for t in range(PACK):
            sg[1].append(gate("sg", y, n1_l, slope1, bias1, t, 1))
        for t in range(PACK):
            sg2[1].append(gate("sg2_", d, n2_l, slope2, bias2, t, 1))
        third_product(0)
        vector_terms(term1, sg, d_bank, 1)
        for t in range(PACK):
            nc.gpsimd.tensor_tensor(term2[1][:, t, :], sg2[1][t][:], y_gain[:, t, :], ALU.mult)

        old_by_vector = tile([P, OLD_PAGES_ON_VECTOR, S], F32, "old_by_vector", reuse="z_bf0")
        old_by_scalar = tile([P, PACK - OLD_PAGES_ON_VECTOR, S], F32, "old_by_scalar", reuse="z0_codes")
        old = []
        for m in range(PACK):
            slots = page[m][:].indirect(n3_l[:])
            if m < OLD_PAGES_ON_VECTOR:
                old.append(old_by_vector[:, m, :])
                nc.vector.tensor_copy(old[m], slots)
            else:
                old.append(old_by_scalar[:, m - OLD_PAGES_ON_VECTOR, :])
                nc.scalar.activation(old[m], slots, ACT.Copy)
        third_product(1)

        for c in range(2):
            for m in range(PACK):
                g, i = divmod(m, 2)
                old_half = old[m][:, half(c)]
                diff = tile([P, HALF], F32, f"diff{c}{m}", reuse=("term2_0", "term1_0")[i])
                nc.vector.tensor_tensor(diff[:], h_bank[c][g][:, i, :], old_half, ALU.subtract)
                step = tile([P, HALF], F32, f"step{c}{m}", reuse=f"step{i}")
                nc.vector.tensor_tensor(step[:], sig_h[c][g][:, i, :], diff[:], ALU.mult)
                slots = page[m][:].indirect(list_half(n3_l, c))
                if m < SCATTER_PAGES_ON_SCALAR[c]:
                    new = tile([P, HALF], F32, f"new{c}{m}")
                    nc.vector.tensor_tensor(new[:], step[:], old_half, ALU.add)
                    nc.scalar.activation(slots, new[:], ACT.Copy)
                else:
                    nc.vector.tensor_tensor(slots, step[:], old_half, ALU.add)
                if c == 1:
                    queue = nc.scalar if m == SCATTER_PAGES_ON_SCALAR[c] - 1 else nc.sync
                    queue.dma_start(out[m * P : (m + 1) * P, :], page[m][:])
